import numpy as np
import ml_dtypes


def mxq(x, axis, fmt="e4m3"):
    dtype, down = {"e4m3": (ml_dtypes.float8_e4m3fn, 7), "e5m2": (ml_dtypes.float8_e5m2, 14)}[fmt]
    v = np.moveaxis(np.asarray(x, np.float32).astype(ml_dtypes.bfloat16).astype(np.float64), axis, -1)
    blocks = v.reshape(v.shape[:-1] + (-1, 32))
    amax = np.abs(blocks).max(-1, keepdims=True)
    byte = np.maximum(np.where(amax > 0, np.frexp(amax)[1] - 1 + 127, 0) - down, 1)
    scale = np.exp2(byte - 127.0)
    codes = (blocks / scale).astype(np.float32).astype(dtype).astype(np.float64)
    return np.moveaxis((codes * scale).reshape(v.shape), -1, axis)


WIDE = False


def mx_kscale(k):
    if not WIDE:
        return np.ones(k)
    levels = np.array([10, -10, 5, -5, 0])
    if k % 512:
        return np.exp2(np.random.permutation(np.resize(levels, k // 32))).repeat(32)
    a = np.empty((k // 512, 16))
    for p in range(k // 512):
        a[p, :8] = np.random.permutation(np.resize(levels, 8))
        for g in range(8):
            far = levels[np.abs(levels - a[p, g]) >= 10]
            a[p, g + 8] = far[np.random.randint(len(far))]
    return np.exp2(a.ravel()).repeat(32)


def f64(x):
    return np.asarray(x).astype(np.float64)


def striped(idx):
    return np.tile(np.asarray(idx).reshape(-1, 16).T, (8, 1)).astype(np.uint16)


def unstriped(offs):
    return offs[:16].T.reshape(-1).astype(np.int64)


E2M1 = np.array([0.0, 0.5, 1.0, 1.5, 2.0, 3.0, 4.0, 6.0, -0.0, -0.5, -1.0, -1.5, -2.0, -3.0, -4.0, -6.0])


def pack_weight(w, fmt):
    k, n = w.shape
    w = f64(np.asarray(w, np.float32).astype(ml_dtypes.bfloat16)).reshape(k // 32, 32, n)
    amax = np.abs(w).max(1)
    if fmt == "e4m3":
        byte = np.frexp(amax)[1] - 1 + 127 - 7
    else:
        mant, ex = np.frexp(amax / 6.0)
        byte = np.where(mant > 0.5, ex, ex - 1) + 127
    byte = np.clip(np.where(amax > 0, byte, 1), 1, 254)
    scaled = (w * np.exp2(127.0 - byte)[:, None, :]).reshape(k, n).astype(np.float32)
    by_word = np.ascontiguousarray(scaled.reshape(k // 512, 128, 4, n).transpose(0, 1, 3, 2))
    if fmt == "e4m3":
        words = by_word.astype(ml_dtypes.float8_e4m3fn).view(np.uint8)
    else:
        c = by_word.astype(ml_dtypes.float4_e2m1fn).view(np.uint8) & 0xF
        words = (c[..., 0::2] | (c[..., 1::2] << 4)).reshape(k // 512, 128, 2 * n)
    return np.ascontiguousarray(words), np.ascontiguousarray(byte.astype(np.uint8).reshape(k // 512, 16, n))


def unpack_weight(words, scales, fmt):
    g, _, n = scales.shape
    words = np.ascontiguousarray(words).reshape(g, 128, n, -1)
    if fmt == "e4m3":
        vals = words.view(ml_dtypes.float8_e4m3fn).astype(np.float64)
    else:
        nib = np.empty((g, 128, n, 4), np.uint8)
        nib[..., 0::2] = words & 0xF
        nib[..., 1::2] = words >> 4
        vals = E2M1[nib]
    vals = vals * np.repeat(np.exp2(scales.astype(np.float64) - 127.0), 8, axis=1)[..., None]
    return vals.transpose(0, 1, 3, 2).reshape(g * 512, n)


D, E, T, I, Q = 512, 512, 2048, 512, 128


def setup_inputs():
    n = np.random.standard_normal
    idx2 = np.random.permutation(I)[:I]
    idx = np.random.permutation(T)[:I]
    fd = mx_kscale(D)
    fe = mx_kscale(E)
    keysp = pack_weight(n((D, T)) / fd[:, None], "e2m1")
    valsp = pack_weight(n((E, T)) / fe[:, None], "e2m1")
    return {
        "query": (n((D, Q)) * 0.8 / np.sqrt(D) * fd[:, None]).astype(np.float32),
        "keys_words": keysp[0],
        "keys_scales": keysp[1],
        "reserve": (np.random.uniform(0.5, 2.0, (Q, 1))).astype(np.float32),
        "gout": (n((E, Q)) * 1 / np.sqrt(E) * fe[:, None]).astype(np.float32),
        "vals_words": valsp[0],
        "vals_scales": valsp[1],
        "dquery": (n((D, Q)) * 1.0 / np.sqrt(D) * fd[:, None]).astype(np.float32),
        "base": (0.5 * n((Q, T))).astype(np.float32),
        "offs2": striped(idx2),
        "offs": striped(idx),
    }


def reference(query, keys_words, keys_scales, reserve, gout, vals_words, vals_scales, dquery, base, offs2, offs):
    idx2 = unstriped(offs2)
    idx = unstriped(offs)
    keysu = unpack_weight(keys_words, keys_scales, "e2m1")
    valsu = unpack_weight(vals_words, vals_scales, "e2m1")
    queryq = mxq(f64(query), 0, "e4m3")
    keysidxg = keysu[:, idx]
    a = queryq.T @ keysidxg
    dqueryq = mxq(f64(dquery), 0, "e4m3")
    ta = dqueryq.T @ keysidxg
    p = np.exp(a)
    z = np.sum(p, axis=1, keepdims=True)
    r = p / (p + p[:, idx2] + f64(reserve))
    goutq = mxq(f64(gout), 0, "e4m3")
    valsidxg = valsu[:, idx]
    c0 = goutq.T @ valsidxg
    dr = c0 * p / z
    dz = np.sum(c0 * r * p / np.square(z) * (-1.0), axis=1, keepdims=True)
    e1 = dr * p / np.square(p + p[:, idx2] + f64(reserve)) * (-1.0)
    s1 = np.zeros((Q, I))
    s1[:, idx2] = e1
    dp = c0 * r / z + dr / (p + p[:, idx2] + f64(reserve)) + dz + s1 - dr * p / np.square(p + p[:, idx2] + f64(reserve))
    tp = ta * p
    tz = np.sum(tp, axis=1, keepdims=True)
    tr = (tp - (tp + tp[:, idx2]) * p / (p + p[:, idx2] + f64(reserve))) / (p + p[:, idx2] + f64(reserve))
    tdr = (tp - tz * p / z) / z * c0
    tdz = np.sum((tr * c0 * p + tp * c0 * r - tz * z * 2.0 * c0 * r * p / np.square(z)) / np.square(z) * (-1.0), axis=1, keepdims=True)
    te1 = (tdr * p + tp * dr - (tp + tp[:, idx2]) * (p + p[:, idx2] + f64(reserve)) * 2.0 * dr * p / np.square(p + p[:, idx2] + f64(reserve))) / np.square(p + p[:, idx2] + f64(reserve)) * (-1.0)
    ts1 = np.zeros((Q, I))
    ts1[:, idx2] = te1
    tdp = (tr * c0 - tz * c0 * r / z) / z + (tdr - (tp + tp[:, idx2]) * dr / (p + p[:, idx2] + f64(reserve))) / (p + p[:, idx2] + f64(reserve)) + tdz + ts1 - (tdr * p + tp * dr - (tp + tp[:, idx2]) * (p + p[:, idx2] + f64(reserve)) * 2.0 * dr * p / np.square(p + p[:, idx2] + f64(reserve))) / np.square(p + p[:, idx2] + f64(reserve))
    tda = tdp * p + tp * dp
    gs = tda * 512.0
    gf = np.zeros((Q, T))
    gf[:, idx] = gs
    y = f64(base) + gf
    return y

@@ -1,0 +1,182 @@
+from contextlib import ExitStack
+
+import concourse.mybir as mybir
+
+D, E, T, I, Q = 512, 512, 2048, 512, 128
+FLOPS = 3 * 2 * Q * D * I
+
+F32 = mybir.dt.float32
+BF16 = mybir.dt.bfloat16
+I32 = mybir.dt.int32
+U32 = mybir.dt.uint32
+U16 = mybir.dt.uint16
+U8 = mybir.dt.uint8
+FP8X4 = mybir.dt.float8_e4m3fn_x4
+FP4X4 = mybir.dt.float4_e2m1fn_x4
+ALU = mybir.AluOpType
+ACT = mybir.ActivationFunctionType
+
+P = 128
+PACK = 4
+HALF = I // 2
+OUT_CHUNK = 512
+
+
+def tile_attend_hvneighbourshare_s_kernel(tc, query, keys_words, keys_scales, reserve, gout, vals_words,
+                                           vals_scales, dquery, base, offs2, offs, out):
+    nc = tc.nc
+    mult, add, sub = ALU.mult, ALU.add, ALU.subtract
+
+    with ExitStack() as ctx:
+        sb = ctx.enter_context(tc.tile_pool(name="sb", bufs=1))
+        ps = ctx.enter_context(tc.psum_pool(name="ps", bufs=1))
+
+        def slots(name, tag=None):
+            return sb.tile([P, I], F32, name=name, tag=tag or name, align_bytes=64)
+
+        def column(name):
+            return sb.tile([P, 1], F32, name=name)
+
+        def halves(lst):
+            cols = HALF // 16
+            return [(slice(h * HALF, (h + 1) * HALF), lst[:, h * cols:(h + 1) * cols]) for h in range(2)]
+
+        tok = sb.tile([P, I // 16], U16, name="tok")
+        link = sb.tile([P, I // 16], U16, name="link")
+        k_words = sb.tile([P, T], U16, name="k_words", align_bytes=64)
+        k_scales = sb.tile([P, T], U8, name="k_scales", align_bytes=64)
+        v_scales = sb.tile([P, T], U8, name="v_scales", align_bytes=64)
+        gf = sb.tile([P, T], F32, name="gf", align_bytes=64)
+        res = column("res")
+
+        nc.vector.memset(k_scales[:, :T // 2].bitcast(I32), 0)
+        nc.gpsimd.memset(k_scales[:, T // 2:].bitcast(I32), 0)
+        nc.vector.memset(v_scales[:].bitcast(I32), 0)
+
+        def load_scales(plane, rows):
+            by_place = rows[0].rearrange("(quad r) t -> r quad t", r=4)
+            for r in range(4):
+                nc.sync.dma_start(out=plane[r:P:32, :].bitcast(I32), in_=by_place[r].bitcast(I32))
+
+        def load_rows(name, src, queue):
+            raw = sb.tile([P, PACK, Q], F32, name=name, align_bytes=64)
+            queue.dma_start(out=raw[:], in_=src.rearrange("(p j) q -> p j q", j=PACK))
+            return raw
+
+        nc.sync.dma_start(tok[:], offs)
+        load_scales(k_scales, keys_scales)
+        q_raw = load_rows("q_raw", query, nc.sync)
+        nc.sync.dma_start(out=k_words[:].bitcast(I32), in_=keys_words[0].bitcast(I32))
+        dq_raw = load_rows("dq_raw", dquery, nc.gpsimd)
+        g_raw = load_rows("g_raw", gout, nc.gpsimd)
+        nc.sync.dma_start(link[:], offs2)
+        load_scales(v_scales, vals_scales)
+        nc.gpsimd.dma_start(out=res[:], in_=reserve)
+        nc.gpsimd.memset(gf[:], 0.0)
+
+        def interleave(name, raw):
+            grouped = sb.tile([P, Q, PACK], BF16, name=name, align_bytes=64)
+            nc.scalar.activation(grouped[:], raw[:].rearrange("p j q -> p q j"), ACT.Copy)
+            return grouped
+
+        def quantise(name, grouped):
+            codes = sb.tile([P, Q], U32, name=name + "_codes", align_bytes=64)
+            scales = sb.tile([P, Q], U8, name=name + "_scales", align_bytes=64)
+            nc.vector.quantize_mx(out=codes[:].bitcast(FP8X4), scales=scales[:],
+                                  in_=grouped[:].rearrange("p q j -> p (q j)"))
+            return codes, scales
+
+        def gather_packed(name, window, dtype):
+            picked = sb.tile([P, I], dtype, name=name, align_bytes=64)
+            nc.vector.tensor_copy(picked[:], window[:].indirect(tok[:]))
+            return picked
+
+        def product(name, rows, words, scales):
+            acc = ps.tile([Q, I], F32, name=name)
+            nc.tensor.matmul_mx(out=acc[:], lhsT=rows[0][:].bitcast(FP8X4), lhsT_scale=rows[1][:],
+                                rhs=words[:].bitcast(FP4X4), rhs_scale=scales[:], start=True, stop=True)
+            return acc
+
+        q_bf = interleave("q_bf", q_raw)
+        dq_bf = interleave("dq_bf", dq_raw)
+        g_bf = interleave("g_bf", g_raw)
+        v_words = sb.tile([P, T], U16, name="v_words", tag="q_raw", align_bytes=64)
+        nc.sync.dma_start(out=v_words[:].bitcast(I32), in_=vals_words[0].bitcast(I32))
+
+        q_mx = quantise("q", q_bf)
+        ks = gather_packed("ks", k_scales, U8)
+        kw = gather_packed("kw", k_words, U16)
+        base_sb = sb.tile([P, T], F32, name="base_sb", tag="k_words", align_bytes=64)
+        nc.sync.dma_start(out=base_sb[:], in_=base)
+        a = product("a", q_mx, kw, ks)
+        dq_mx = quantise("dq", dq_bf)
+        ta = product("ta", dq_mx, kw, ks)
+
+        p, z = slots("p"), column("z")
+        nc.scalar.activation(p[:], a[:], ACT.Exp, accum_out=z[:])
+        p2 = slots("p2")
+        for cols, entries in halves(link):
+            nc.scalar.activation(p2[:, cols], p[:].indirect(entries), ACT.Copy)
+
+        vs = gather_packed("vs", v_scales, U8)
+        vw = gather_packed("vw", v_words, U16)
+        den = slots("den")
+        nc.vector.scalar_tensor_tensor(den[:], p2[:], res[:], p[:], add, add)
+        tp, tz = slots("tp"), column("tz")
+        nc.vector.scalar_tensor_tensor(tp[:], ta[:], 1.0, p[:], mult, mult, accum_out=tz[:])
+        g_mx = quantise("g", g_bf)
+        c0 = product("c0", g_mx, vw, vs)
+
+        zi, m, m2, hz = column("zi"), column("m"), column("m2"), column("hz")
+        nc.vector.reciprocal(zi[:], z[:])
+        x = slots("x")
+        nc.vector.scalar_tensor_tensor(x[:], p2[:], res[:], ta[:], add, mult)
+        nc.vector.tensor_scalar(m[:], tz[:], zi[:], None, mult)
+        nc.vector.tensor_scalar(m2[:], tz[:], zi[:], 2.0, mult, mult)
+        nc.vector.tensor_scalar(hz[:], zi[:], -0.5, None, mult)
+
+        rs, u, t, t2 = slots("rs"), slots("u"), slots("t", "q_raw"), slots("t2")
+        nc.scalar.activation(rs[:], den[:], ACT.Abs_reciprocal_sqrt)
+        nc.vector.tensor_tensor(t[:], p[:], rs[:], mult)
+        nc.scalar.activation(u[:], rs[:], ACT.Square)
+        nc.scalar.activation(t2[:], t[:], ACT.Square)
+        tp2 = slots("tp2", "q_raw")
+        for cols, entries in halves(link):
+            nc.scalar.activation(tp2[:, cols], tp[:].indirect(entries), ACT.Copy)
+
+        gp, sum_gp = slots("gp"), column("sum_gp")
+        e1, s1 = slots("e1"), slots("s1")
+        y, v2, te1, ts1 = slots("y"), slots("v2"), slots("te1"), slots("ts1")
+        dz, mdz, tdz = column("dz"), column("mdz"), column("tdz")
+        n2, q2, sum_q2 = slots("n2"), slots("q2"), column("sum_q2")
+        b2, f1, g1, f0 = (slots(n) for n in ("b2", "f1", "g1", "f0"))
+
+        nc.vector.scalar_tensor_tensor(gp[:], c0[:], zi[:], t2[:], mult, mult, accum_out=sum_gp[:])
+        for cols, entries in halves(link):
+            nc.vector.scalar_tensor_tensor(e1[:, cols], gp[:, cols], -1.0, u[:, cols], mult, mult)
+            nc.scalar.activation(s1[:].indirect(entries), e1[:, cols], ACT.Copy)
+        nc.vector.tensor_tensor(y[:], x[:], tp2[:], sub)
+        nc.vector.tensor_scalar(dz[:], sum_gp[:], zi[:], -1.0, mult, mult)
+        nc.vector.scalar_tensor_tensor(v2[:], y[:], 2.0, u[:], mult, mult)
+        nc.vector.tensor_scalar(mdz[:], dz[:], m[:], None, mult)
+        nc.vector.scalar_tensor_tensor(n2[:], ta[:], 2.0, v2[:], mult, add)
+        nc.vector.scalar_tensor_tensor(te1[:], v2[:], m[:], e1[:], sub, mult)
+        for cols, entries in halves(link):
+            nc.scalar.activation(ts1[:].indirect(entries), te1[:, cols], ACT.Copy)
+        nc.vector.scalar_tensor_tensor(q2[:], n2[:], m2[:], gp[:], sub, mult, accum_out=sum_q2[:])
+        nc.vector.tensor_scalar(tdz[:], sum_q2[:], hz[:], mdz[:], mult, sub)
+        nc.vector.scalar_tensor_tensor(g1[:], te1[:], tdz[:], p[:], add, mult)
+        a2 = slots("a2", "n2")
+        nc.vector.scalar_tensor_tensor(a2[:], s1[:], dz[:], e1[:], add, add)
+        nc.vector.tensor_tensor(f1[:], q2[:], g1[:], add)
+        nc.vector.scalar_tensor_tensor(b2[:], a2[:], 512.0, tp[:], mult, mult)
+        nc.vector.scalar_tensor_tensor(f0[:], f1[:], 512.0, b2[:], mult, add)
+        b1 = slots("b1", "f1")
+        nc.vector.scalar_tensor_tensor(b1[:], ts1[:], 512.0, p[:], mult, mult)
+        nc.vector.tensor_tensor(gf[:].indirect(tok[:]), b1[:], f0[:], add)
+
+        for c in range(T // OUT_CHUNK):
+            cols = slice(c * OUT_CHUNK, (c + 1) * OUT_CHUNK)
+            done = sb.tile([P, OUT_CHUNK], F32, name=f"done{c}")
+            nc.vector.tensor_tensor(done[:], gf[:, cols], base_sb[:, cols], add)
+            nc.sync.dma_start(out=out[:, cols], in_=done[:])

@@ -44,19 +44,18 @@ def tile_attend_hvneighbourshare_s_kernel(tc, query, keys_words, keys_scales, re
         tok = sb.tile([P, I // 16], U16, name="tok")
         link = sb.tile([P, I // 16], U16, name="link")
         k_words = sb.tile([P, T], U16, name="k_words", align_bytes=64)
+        v_words = sb.tile([P, T], U16, name="v_words", align_bytes=64)
         k_scales = sb.tile([P, T], U8, name="k_scales", align_bytes=64)
         v_scales = sb.tile([P, T], U8, name="v_scales", align_bytes=64)
-        gf = sb.tile([P, T], F32, name="gf", align_bytes=64)
         res = column("res")
 
-        nc.vector.memset(k_scales[:, :T // 2].bitcast(I32), 0)
-        nc.gpsimd.memset(k_scales[:, T // 2:].bitcast(I32), 0)
+        nc.vector.memset(k_scales[:].bitcast(I32), 0)
         nc.vector.memset(v_scales[:].bitcast(I32), 0)
 
-        def load_scales(plane, rows):
+        def load_scales(plane, rows, queue):
             by_place = rows[0].rearrange("(quad r) t -> r quad t", r=4)
             for r in range(4):
-                nc.sync.dma_start(out=plane[r:P:32, :].bitcast(I32), in_=by_place[r].bitcast(I32))
+                queue.dma_start(out=plane[r:P:32, :].bitcast(I32), in_=by_place[r].bitcast(I32))
 
         def load_rows(name, src, queue):
             raw = sb.tile([P, PACK, Q], F32, name=name, align_bytes=64)
@@ -64,30 +63,30 @@ def tile_attend_hvneighbourshare_s_kernel(tc, query, keys_words, keys_scales, re
             return raw
 
         nc.sync.dma_start(tok[:], offs)
-        load_scales(k_scales, keys_scales)
-        q_raw = load_rows("q_raw", query, nc.sync)
+        load_scales(k_scales, keys_scales, nc.scalar)
+        q_raw = load_rows("q_raw", query, nc.gpsimd)
         nc.sync.dma_start(out=k_words[:].bitcast(I32), in_=keys_words[0].bitcast(I32))
         dq_raw = load_rows("dq_raw", dquery, nc.gpsimd)
         g_raw = load_rows("g_raw", gout, nc.gpsimd)
+        nc.sync.dma_start(out=v_words[:].bitcast(I32), in_=vals_words[0].bitcast(I32))
         nc.sync.dma_start(link[:], offs2)
-        load_scales(v_scales, vals_scales)
+        load_scales(v_scales, vals_scales, nc.sync)
         nc.gpsimd.dma_start(out=res[:], in_=reserve)
-        nc.gpsimd.memset(gf[:], 0.0)
 
-        def interleave(name, raw):
-            grouped = sb.tile([P, Q, PACK], BF16, name=name, align_bytes=64)
+        def interleave(name, raw, tag):
+            grouped = sb.tile([P, Q, PACK], BF16, name=name, tag=tag, align_bytes=64)
             nc.scalar.activation(grouped[:], raw[:].rearrange("p j q -> p q j"), ACT.Copy)
             return grouped
 
-        def quantise(name, grouped):
-            codes = sb.tile([P, Q], U32, name=name + "_codes", align_bytes=64)
+        def quantise(name, grouped, tag=None):
+            codes = sb.tile([P, Q], U32, name=name + "_codes", tag=tag or name + "_codes", align_bytes=64)
             scales = sb.tile([P, Q], U8, name=name + "_scales", align_bytes=64)
             nc.vector.quantize_mx(out=codes[:].bitcast(FP8X4), scales=scales[:],
                                   in_=grouped[:].rearrange("p q j -> p (q j)"))
             return codes, scales
 
-        def gather_packed(name, window, dtype):
-            picked = sb.tile([P, I], dtype, name=name, align_bytes=64)
+        def gather_packed(name, window, dtype, tag=None):
+            picked = sb.tile([P, I], dtype, name=name, tag=tag or name, align_bytes=64)
             nc.vector.tensor_copy(picked[:], window[:].indirect(tok[:]))
             return picked
 
@@ -97,66 +96,67 @@ def tile_attend_hvneighbourshare_s_kernel(tc, query, keys_words, keys_scales, re
                                 rhs=words[:].bitcast(FP4X4), rhs_scale=scales[:], start=True, stop=True)
             return acc
 
-        q_bf = interleave("q_bf", q_raw)
-        dq_bf = interleave("dq_bf", dq_raw)
-        g_bf = interleave("g_bf", g_raw)
-        v_words = sb.tile([P, T], U16, name="v_words", tag="q_raw", align_bytes=64)
-        nc.sync.dma_start(out=v_words[:].bitcast(I32), in_=vals_words[0].bitcast(I32))
+        q_bf = interleave("q_bf", q_raw, "q_bf")
+        dq_bf = interleave("dq_bf", dq_raw, "q_raw")
+        g_bf = interleave("g_bf", g_raw, "dq_raw")
 
         q_mx = quantise("q", q_bf)
-        ks = gather_packed("ks", k_scales, U8)
         kw = gather_packed("kw", k_words, U16)
+        ks = gather_packed("ks", k_scales, U8)
+        a = product("a", q_mx, kw, ks)
+        dq_mx = quantise("dq", dq_bf, "k_words")
+        ta = product("ta", dq_mx, kw, ks)
         base_sb = sb.tile([P, T], F32, name="base_sb", tag="k_words", align_bytes=64)
         nc.sync.dma_start(out=base_sb[:], in_=base)
-        a = product("a", q_mx, kw, ks)
-        dq_mx = quantise("dq", dq_bf)
-        ta = product("ta", dq_mx, kw, ks)
 
-        p, z = slots("p"), column("z")
+        p, z = slots("p", "g_raw"), column("z")
         nc.scalar.activation(p[:], a[:], ACT.Exp, accum_out=z[:])
         p2 = slots("p2")
         for cols, entries in halves(link):
             nc.scalar.activation(p2[:, cols], p[:].indirect(entries), ACT.Copy)
 
-        vs = gather_packed("vs", v_scales, U8)
-        vw = gather_packed("vw", v_words, U16)
-        den = slots("den")
-        nc.vector.scalar_tensor_tensor(den[:], p2[:], res[:], p[:], add, add)
-        tp, tz = slots("tp"), column("tz")
+        vw = gather_packed("vw", v_words, U16, "k_scales")
+        tp, tz, tp2 = slots("tp"), column("tz"), slots("tp2")
         nc.vector.scalar_tensor_tensor(tp[:], ta[:], 1.0, p[:], mult, mult, accum_out=tz[:])
+        for cols, entries in halves(link):
+            nc.scalar.activation(tp2[:, cols], tp[:].indirect(entries), ACT.Copy)
         g_mx = quantise("g", g_bf)
+        gf = sb.tile([P, T], F32, name="gf", tag="dq_raw", align_bytes=64)
+        nc.gpsimd.memset(gf[:], 0.0)
+        vs = gather_packed("vs", v_scales, U8)
         c0 = product("c0", g_mx, vw, vs)
+        den = slots("den", "v_scales")
+        nc.vector.scalar_tensor_tensor(den[:], p2[:], res[:], p[:], add, add)
 
-        zi, m, m2, hz = column("zi"), column("m"), column("m2"), column("hz")
-        nc.vector.reciprocal(zi[:], z[:])
-        x = slots("x")
+        zi, nzi, m, m2, hz = (column(n) for n in ("zi", "nzi", "m", "m2", "hz"))
+        x, y = slots("x", "g_codes"), slots("y")
         nc.vector.scalar_tensor_tensor(x[:], p2[:], res[:], ta[:], add, mult)
+        nc.vector.reciprocal(zi[:], z[:])
+        nc.vector.tensor_tensor(y[:], x[:], tp2[:], sub)
         nc.vector.tensor_scalar(m[:], tz[:], zi[:], None, mult)
         nc.vector.tensor_scalar(m2[:], tz[:], zi[:], 2.0, mult, mult)
         nc.vector.tensor_scalar(hz[:], zi[:], -0.5, None, mult)
+        nc.vector.tensor_scalar(nzi[:], zi[:], -1.0, None, mult)
 
-        rs, u, t, t2 = slots("rs"), slots("u"), slots("t", "q_raw"), slots("t2")
-        nc.scalar.activation(rs[:], den[:], ACT.Abs_reciprocal_sqrt)
-        nc.vector.tensor_tensor(t[:], p[:], rs[:], mult)
-        nc.scalar.activation(u[:], rs[:], ACT.Square)
-        nc.scalar.activation(t2[:], t[:], ACT.Square)
-        tp2 = slots("tp2", "q_raw")
-        for cols, entries in halves(link):
-            nc.scalar.activation(tp2[:, cols], tp[:].indirect(entries), ACT.Copy)
-
-        gp, sum_gp = slots("gp"), column("sum_gp")
+        rs, u, t, t2 = slots("rs"), slots("u"), slots("t"), slots("t2")
+        gp, sum_gp = slots("gp"), [column("sum_gp0"), column("sum_gp1")]
         e1, s1 = slots("e1"), slots("s1")
-        y, v2, te1, ts1 = slots("y"), slots("v2"), slots("te1"), slots("ts1")
+        v2, te1, ts1 = slots("v2"), slots("te1"), slots("ts1")
         dz, mdz, tdz = column("dz"), column("mdz"), column("tdz")
         n2, q2, sum_q2 = slots("n2"), slots("q2"), column("sum_q2")
         b2, f1, g1, f0 = (slots(n) for n in ("b2", "f1", "g1", "f0"))
 
-        nc.vector.scalar_tensor_tensor(gp[:], c0[:], zi[:], t2[:], mult, mult, accum_out=sum_gp[:])
         for cols, entries in halves(link):
+            nc.scalar.activation(rs[:, cols], den[:, cols], ACT.Abs_reciprocal_sqrt)
+            nc.vector.tensor_tensor(t[:, cols], p[:, cols], rs[:, cols], mult)
+        for (cols, entries), part in zip(halves(link), sum_gp):
+            nc.scalar.activation(t2[:, cols], t[:, cols], ACT.Square)
+            nc.scalar.activation(u[:, cols], rs[:, cols], ACT.Square)
+            nc.vector.scalar_tensor_tensor(gp[:, cols], c0[:, cols], zi[:], t2[:, cols], mult, mult, accum_out=part[:])
             nc.vector.scalar_tensor_tensor(e1[:, cols], gp[:, cols], -1.0, u[:, cols], mult, mult)
+        for cols, entries in halves(link):
             nc.scalar.activation(s1[:].indirect(entries), e1[:, cols], ACT.Copy)
-        nc.vector.tensor_tensor(y[:], x[:], tp2[:], sub)
-        nc.vector.tensor_scalar(dz[:], sum_gp[:], zi[:], -1.0, mult, mult)
+        nc.vector.tensor_scalar(dz[:], sum_gp[0][:], sum_gp[1][:], nzi[:], add, mult)
         nc.vector.scalar_tensor_tensor(v2[:], y[:], 2.0, u[:], mult, mult)
         nc.vector.tensor_scalar(mdz[:], dz[:], m[:], None, mult)
         nc.vector.scalar_tensor_tensor(n2[:], ta[:], 2.0, v2[:], mult, add)

@@ -19,7 +19,7 @@ ACT = mybir.ActivationFunctionType
 P = 128
 PACK = 4
 HALF = I // 2
-OUT_CHUNK = 512
+OUT_EDGES = (0, 256, 768, 1280, 1792, 2048)
 
 
 def tile_attend_hvneighbourshare_s_kernel(tc, query, keys_words, keys_scales, reserve, gout, vals_words,
@@ -63,14 +63,14 @@ def tile_attend_hvneighbourshare_s_kernel(tc, query, keys_words, keys_scales, re
             return raw
 
         nc.sync.dma_start(tok[:], offs)
-        load_scales(k_scales, keys_scales, nc.scalar)
-        q_raw = load_rows("q_raw", query, nc.gpsimd)
-        nc.sync.dma_start(out=k_words[:].bitcast(I32), in_=keys_words[0].bitcast(I32))
-        dq_raw = load_rows("dq_raw", dquery, nc.gpsimd)
-        g_raw = load_rows("g_raw", gout, nc.gpsimd)
-        nc.sync.dma_start(out=v_words[:].bitcast(I32), in_=vals_words[0].bitcast(I32))
         nc.sync.dma_start(link[:], offs2)
+        load_scales(k_scales, keys_scales, nc.scalar)
+        nc.sync.dma_start(out=k_words[:].bitcast(I32), in_=keys_words[0].bitcast(I32))
+        q_raw = load_rows("q_raw", query, nc.sync)
+        dq_raw = load_rows("dq_raw", dquery, nc.sync)
+        nc.sync.dma_start(out=v_words[:].bitcast(I32), in_=vals_words[0].bitcast(I32))
         load_scales(v_scales, vals_scales, nc.sync)
+        g_raw = load_rows("g_raw", gout, nc.gpsimd)
         nc.gpsimd.dma_start(out=res[:], in_=reserve)
 
         def interleave(name, raw, tag):
@@ -100,9 +100,9 @@ def tile_attend_hvneighbourshare_s_kernel(tc, query, keys_words, keys_scales, re
         dq_bf = interleave("dq_bf", dq_raw, "q_raw")
         g_bf = interleave("g_bf", g_raw, "dq_raw")
 
-        q_mx = quantise("q", q_bf)
         kw = gather_packed("kw", k_words, U16)
-        ks = gather_packed("ks", k_scales, U8)
+        q_mx = quantise("q", q_bf)
+        ks = gather_packed("ks", k_scales, U8, "q_bf")
         a = product("a", q_mx, kw, ks)
         dq_mx = quantise("dq", dq_bf, "k_words")
         ta = product("ta", dq_mx, kw, ks)
@@ -116,58 +116,64 @@ def tile_attend_hvneighbourshare_s_kernel(tc, query, keys_words, keys_scales, re
             nc.scalar.activation(p2[:, cols], p[:].indirect(entries), ACT.Copy)
 
         vw = gather_packed("vw", v_words, U16, "k_scales")
-        tp, tz, tp2 = slots("tp"), column("tz"), slots("tp2")
-        nc.vector.scalar_tensor_tensor(tp[:], ta[:], 1.0, p[:], mult, mult, accum_out=tz[:])
-        for cols, entries in halves(link):
-            nc.scalar.activation(tp2[:, cols], tp[:].indirect(entries), ACT.Copy)
         g_mx = quantise("g", g_bf)
-        gf = sb.tile([P, T], F32, name="gf", tag="dq_raw", align_bytes=64)
-        nc.gpsimd.memset(gf[:], 0.0)
-        vs = gather_packed("vs", v_scales, U8)
+        vs = gather_packed("vs", v_scales, U8, "v_words")
         c0 = product("c0", g_mx, vw, vs)
+        gf = sb.tile([P, T], F32, name="gf", tag="v_words", align_bytes=64)
+        nc.gpsimd.memset(gf[:], 0.0)
         den = slots("den", "v_scales")
         nc.vector.scalar_tensor_tensor(den[:], p2[:], res[:], p[:], add, add)
+        tp, tz = slots("tp"), column("tz")
+        nc.vector.scalar_tensor_tensor(tp[:], ta[:], 1.0, p[:], mult, mult, accum_out=tz[:])
 
-        zi, nzi, m, m2, hz = (column(n) for n in ("zi", "nzi", "m", "m2", "hz"))
-        x, y = slots("x", "g_codes"), slots("y")
+        zi, m, m2, hz = (column(n) for n in ("zi", "m", "m2", "hz"))
+        x = slots("x", "g_codes")
         nc.vector.scalar_tensor_tensor(x[:], p2[:], res[:], ta[:], add, mult)
         nc.vector.reciprocal(zi[:], z[:])
-        nc.vector.tensor_tensor(y[:], x[:], tp2[:], sub)
         nc.vector.tensor_scalar(m[:], tz[:], zi[:], None, mult)
         nc.vector.tensor_scalar(m2[:], tz[:], zi[:], 2.0, mult, mult)
-        nc.vector.tensor_scalar(hz[:], zi[:], -0.5, None, mult)
-        nc.vector.tensor_scalar(nzi[:], zi[:], -1.0, None, mult)
+        nc.vector.tensor_scalar(hz[:], zi[:], 0.5, None, mult)
 
-        rs, u, t, t2 = slots("rs"), slots("u"), slots("t"), slots("t2")
+        rs, u, t = slots("rs"), slots("u"), slots("t")
         gp, sum_gp = slots("gp"), [column("sum_gp0"), column("sum_gp1")]
         e1, s1 = slots("e1"), slots("s1")
         v2, te1, ts1 = slots("v2"), slots("te1"), slots("ts1")
-        dz, mdz, tdz = column("dz"), column("mdz"), column("tdz")
+        ndz, mndz, ntdz = column("ndz"), column("mndz"), column("ntdz")
         n2, q2, sum_q2 = slots("n2"), slots("q2"), column("sum_q2")
         b2, f1, g1, f0 = (slots(n) for n in ("b2", "f1", "g1", "f0"))
 
+        def half_tile(name, tag):
+            return sb.tile([P, HALF], F32, name=name, tag=tag, align_bytes=64)
+
+        (cols0, entries0), (cols1, entries1) = halves(link)
         for cols, entries in halves(link):
             nc.scalar.activation(rs[:, cols], den[:, cols], ACT.Abs_reciprocal_sqrt)
             nc.vector.tensor_tensor(t[:, cols], p[:, cols], rs[:, cols], mult)
-        for (cols, entries), part in zip(halves(link), sum_gp):
-            nc.scalar.activation(t2[:, cols], t[:, cols], ACT.Square)
+        for h, (cols, entries) in enumerate(halves(link)):
+            t2 = half_tile(f"t2_{h}", f"t2_{h}")
+            nc.scalar.activation(t2[:], t[:, cols], ACT.Square)
             nc.scalar.activation(u[:, cols], rs[:, cols], ACT.Square)
-            nc.vector.scalar_tensor_tensor(gp[:, cols], c0[:, cols], zi[:], t2[:, cols], mult, mult, accum_out=part[:])
+            nc.vector.scalar_tensor_tensor(gp[:, cols], c0[:, cols], zi[:], t2[:], mult, mult, accum_out=sum_gp[h][:])
             nc.vector.scalar_tensor_tensor(e1[:, cols], gp[:, cols], -1.0, u[:, cols], mult, mult)
         for cols, entries in halves(link):
             nc.scalar.activation(s1[:].indirect(entries), e1[:, cols], ACT.Copy)
-        nc.vector.tensor_scalar(dz[:], sum_gp[0][:], sum_gp[1][:], nzi[:], add, mult)
-        nc.vector.scalar_tensor_tensor(v2[:], y[:], 2.0, u[:], mult, mult)
-        nc.vector.tensor_scalar(mdz[:], dz[:], m[:], None, mult)
-        nc.vector.scalar_tensor_tensor(n2[:], ta[:], 2.0, v2[:], mult, add)
-        nc.vector.scalar_tensor_tensor(te1[:], v2[:], m[:], e1[:], sub, mult)
+        ny0 = half_tile("ny0", "t2_0")
+        nc.vector.tensor_tensor(ny0[:], tp[:].indirect(entries0), x[:, cols0], sub)
+        ny1 = half_tile("ny1", "t2_1")
+        nc.vector.tensor_tensor(ny1[:], tp[:].indirect(entries1), x[:, cols1], sub)
+        nc.vector.scalar_tensor_tensor(v2[:, cols0], ny0[:], -2.0, u[:, cols0], mult, mult)
+        nc.vector.scalar_tensor_tensor(v2[:, cols1], ny1[:], -2.0, u[:, cols1], mult, mult)
         for cols, entries in halves(link):
+            nc.vector.scalar_tensor_tensor(te1[:, cols], v2[:, cols], m[:], e1[:, cols], sub, mult)
             nc.scalar.activation(ts1[:].indirect(entries), te1[:, cols], ACT.Copy)
+        nc.vector.tensor_scalar(ndz[:], sum_gp[0][:], sum_gp[1][:], zi[:], add, mult)
+        nc.vector.scalar_tensor_tensor(n2[:], ta[:], 2.0, v2[:], mult, add)
+        nc.vector.tensor_scalar(mndz[:], ndz[:], m[:], None, mult)
         nc.vector.scalar_tensor_tensor(q2[:], n2[:], m2[:], gp[:], sub, mult, accum_out=sum_q2[:])
-        nc.vector.tensor_scalar(tdz[:], sum_q2[:], hz[:], mdz[:], mult, sub)
-        nc.vector.scalar_tensor_tensor(g1[:], te1[:], tdz[:], p[:], add, mult)
+        nc.vector.tensor_scalar(ntdz[:], sum_q2[:], hz[:], mndz[:], mult, sub)
+        nc.vector.scalar_tensor_tensor(g1[:], te1[:], ntdz[:], p[:], sub, mult)
         a2 = slots("a2", "n2")
-        nc.vector.scalar_tensor_tensor(a2[:], s1[:], dz[:], e1[:], add, add)
+        nc.vector.scalar_tensor_tensor(a2[:], s1[:], ndz[:], e1[:], sub, add)
         nc.vector.tensor_tensor(f1[:], q2[:], g1[:], add)
         nc.vector.scalar_tensor_tensor(b2[:], a2[:], 512.0, tp[:], mult, mult)
         nc.vector.scalar_tensor_tensor(f0[:], f1[:], 512.0, b2[:], mult, add)
@@ -175,8 +181,8 @@ def tile_attend_hvneighbourshare_s_kernel(tc, query, keys_words, keys_scales, re
         nc.vector.scalar_tensor_tensor(b1[:], ts1[:], 512.0, p[:], mult, mult)
         nc.vector.tensor_tensor(gf[:].indirect(tok[:]), b1[:], f0[:], add)
 
-        for c in range(T // OUT_CHUNK):
-            cols = slice(c * OUT_CHUNK, (c + 1) * OUT_CHUNK)
-            done = sb.tile([P, OUT_CHUNK], F32, name=f"done{c}")
+        for c, (lo, hi) in enumerate(zip(OUT_EDGES, OUT_EDGES[1:])):
+            cols = slice(lo, hi)
+            done = sb.tile([P, hi - lo], F32, name=f"done{c}")
             nc.vector.tensor_tensor(done[:], gf[:, cols], base_sb[:, cols], add)
             nc.sync.dma_start(out=out[:, cols], in_=done[:])

@@ -126,15 +126,15 @@ def tile_attend_hvneighbourshare_s_kernel(tc, query, keys_words, keys_scales, re
         tp, tz = slots("tp"), column("tz")
         nc.vector.scalar_tensor_tensor(tp[:], ta[:], 1.0, p[:], mult, mult, accum_out=tz[:])
 
-        zi, m, m2, hz = (column(n) for n in ("zi", "m", "m2", "hz"))
-        x = slots("x", "g_codes")
-        nc.vector.scalar_tensor_tensor(x[:], p2[:], res[:], ta[:], add, mult)
+        zi, hz = column("zi"), column("hz")
         nc.vector.reciprocal(zi[:], z[:])
-        nc.vector.tensor_scalar(m[:], tz[:], zi[:], None, mult)
-        nc.vector.tensor_scalar(m2[:], tz[:], zi[:], 2.0, mult, mult)
+        dr, x, drp = slots("dr"), slots("x", "g_codes"), slots("drp")
+        nc.vector.scalar_tensor_tensor(dr[:], c0[:], zi[:], p[:], mult, mult)
+        nc.vector.scalar_tensor_tensor(x[:], p2[:], res[:], ta[:], add, mult)
+        nc.vector.tensor_tensor(drp[:], dr[:], p[:], mult)
         nc.vector.tensor_scalar(hz[:], zi[:], 0.5, None, mult)
 
-        rs, u, t = slots("rs"), slots("u"), slots("t")
+        rs, u = slots("rs"), slots("u")
         gp, sum_gp = slots("gp"), [column("sum_gp0"), column("sum_gp1")]
         e1, s1 = slots("e1"), slots("s1")
         v2, te1, ts1 = slots("v2"), slots("te1"), slots("ts1")
@@ -142,40 +142,39 @@ def tile_attend_hvneighbourshare_s_kernel(tc, query, keys_words, keys_scales, re
         n2, q2, sum_q2 = slots("n2"), slots("q2"), column("sum_q2")
         b2, f1, g1, f0 = (slots(n) for n in ("b2", "f1", "g1", "f0"))
 
-        def half_tile(name, tag):
-            return sb.tile([P, HALF], F32, name=name, tag=tag, align_bytes=64)
-
-        (cols0, entries0), (cols1, entries1) = halves(link)
         for cols, entries in halves(link):
             nc.scalar.activation(rs[:, cols], den[:, cols], ACT.Abs_reciprocal_sqrt)
-            nc.vector.tensor_tensor(t[:, cols], p[:, cols], rs[:, cols], mult)
-        for h, (cols, entries) in enumerate(halves(link)):
-            t2 = half_tile(f"t2_{h}", f"t2_{h}")
-            nc.scalar.activation(t2[:], t[:, cols], ACT.Square)
-            nc.scalar.activation(u[:, cols], rs[:, cols], ACT.Square)
-            nc.vector.scalar_tensor_tensor(gp[:, cols], c0[:, cols], zi[:], t2[:], mult, mult, accum_out=sum_gp[h][:])
-            nc.vector.scalar_tensor_tensor(e1[:, cols], gp[:, cols], -1.0, u[:, cols], mult, mult)
         for cols, entries in halves(link):
+            nc.scalar.activation(u[:, cols], rs[:, cols], ACT.Square)
+        (cols0, entries0), (cols1, entries1) = halves(link)
+        tp2 = sb.tile([P, HALF], F32, name="tp2", tag="rs", align_bytes=64)
+        nc.scalar.activation(tp2[:], tp[:].indirect(entries0), ACT.Copy)
+        for h, (cols, entries) in enumerate(halves(link)):
+            nc.vector.scalar_tensor_tensor(gp[:, cols], drp[:, cols], 1.0, u[:, cols], mult, mult, accum_out=sum_gp[h][:])
+        for cols, entries in halves(link):
+            nc.vector.scalar_tensor_tensor(e1[:, cols], gp[:, cols], -1.0, u[:, cols], mult, mult)
             nc.scalar.activation(s1[:].indirect(entries), e1[:, cols], ACT.Copy)
-        ny0 = half_tile("ny0", "t2_0")
-        nc.vector.tensor_tensor(ny0[:], tp[:].indirect(entries0), x[:, cols0], sub)
-        ny1 = half_tile("ny1", "t2_1")
-        nc.vector.tensor_tensor(ny1[:], tp[:].indirect(entries1), x[:, cols1], sub)
-        nc.vector.scalar_tensor_tensor(v2[:, cols0], ny0[:], -2.0, u[:, cols0], mult, mult)
-        nc.vector.scalar_tensor_tensor(v2[:, cols1], ny1[:], -2.0, u[:, cols1], mult, mult)
+        m, m2 = column("m"), column("m2")
+        nc.vector.tensor_tensor(m[:], tz[:], zi[:], mult)
+        ny = slots("ny", "drp")
+        nc.vector.tensor_tensor(ny[:, cols0], tp2[:], x[:, cols0], sub)
+        nc.vector.tensor_tensor(ny[:, cols1], tp[:].indirect(entries1), x[:, cols1], sub)
+        nc.vector.tensor_tensor(m2[:], m[:], m[:], add)
+        nc.vector.tensor_scalar(ndz[:], sum_gp[0][:], sum_gp[1][:], zi[:], add, mult)
+        for cols, entries in halves(link):
+            nc.vector.scalar_tensor_tensor(v2[:, cols], ny[:, cols], -2.0, u[:, cols], mult, mult)
         for cols, entries in halves(link):
             nc.vector.scalar_tensor_tensor(te1[:, cols], v2[:, cols], m[:], e1[:, cols], sub, mult)
             nc.scalar.activation(ts1[:].indirect(entries), te1[:, cols], ACT.Copy)
-        nc.vector.tensor_scalar(ndz[:], sum_gp[0][:], sum_gp[1][:], zi[:], add, mult)
         nc.vector.scalar_tensor_tensor(n2[:], ta[:], 2.0, v2[:], mult, add)
         nc.vector.tensor_scalar(mndz[:], ndz[:], m[:], None, mult)
         nc.vector.scalar_tensor_tensor(q2[:], n2[:], m2[:], gp[:], sub, mult, accum_out=sum_q2[:])
         nc.vector.tensor_scalar(ntdz[:], sum_q2[:], hz[:], mndz[:], mult, sub)
-        nc.vector.scalar_tensor_tensor(g1[:], te1[:], ntdz[:], p[:], sub, mult)
         a2 = slots("a2", "n2")
         nc.vector.scalar_tensor_tensor(a2[:], s1[:], ndz[:], e1[:], sub, add)
-        nc.vector.tensor_tensor(f1[:], q2[:], g1[:], add)
+        nc.vector.scalar_tensor_tensor(g1[:], te1[:], ntdz[:], p[:], sub, mult)
         nc.vector.scalar_tensor_tensor(b2[:], a2[:], 512.0, tp[:], mult, mult)
+        nc.vector.tensor_tensor(f1[:], q2[:], g1[:], add)
         nc.vector.scalar_tensor_tensor(f0[:], f1[:], 512.0, b2[:], mult, add)
         b1 = slots("b1", "f1")
         nc.vector.scalar_tensor_tensor(b1[:], ts1[:], 512.0, p[:], mult, mult)

from contextlib import ExitStack

import concourse.mybir as mybir

D, E, T, I, Q = 512, 512, 2048, 512, 128
FLOPS = 3 * 2 * Q * D * I

F32 = mybir.dt.float32
BF16 = mybir.dt.bfloat16
I32 = mybir.dt.int32
U32 = mybir.dt.uint32
U16 = mybir.dt.uint16
U8 = mybir.dt.uint8
FP8X4 = mybir.dt.float8_e4m3fn_x4
FP4X4 = mybir.dt.float4_e2m1fn_x4
ALU = mybir.AluOpType
ACT = mybir.ActivationFunctionType

P = 128
PACK = 4
HALF = I // 2
OUT_EDGES = (0, 256, 768, 1280, 1792, 2048)


def tile_attend_hvneighbourshare_s_kernel(tc, query, keys_words, keys_scales, reserve, gout, vals_words,
                                           vals_scales, dquery, base, offs2, offs, out):
    nc = tc.nc
    mult, add, sub = ALU.mult, ALU.add, ALU.subtract

    with ExitStack() as ctx:
        sb = ctx.enter_context(tc.tile_pool(name="sb", bufs=1))
        ps = ctx.enter_context(tc.psum_pool(name="ps", bufs=1))

        def slots(name, tag=None):
            return sb.tile([P, I], F32, name=name, tag=tag or name, align_bytes=64)

        def column(name):
            return sb.tile([P, 1], F32, name=name)

        def halves(lst):
            cols = HALF // 16
            return [(slice(h * HALF, (h + 1) * HALF), lst[:, h * cols:(h + 1) * cols]) for h in range(2)]

        tok = sb.tile([P, I // 16], U16, name="tok")
        link = sb.tile([P, I // 16], U16, name="link")
        k_words = sb.tile([P, T], U16, name="k_words", align_bytes=64)
        v_words = sb.tile([P, T], U16, name="v_words", align_bytes=64)
        k_scales = sb.tile([P, T], U8, name="k_scales", align_bytes=64)
        v_scales = sb.tile([P, T], U8, name="v_scales", align_bytes=64)
        res = column("res")

        nc.vector.memset(k_scales[:].bitcast(I32), 0)
        nc.vector.memset(v_scales[:].bitcast(I32), 0)

        def load_scales(plane, rows, queue):
            by_place = rows[0].rearrange("(quad r) t -> r quad t", r=4)
            for r in range(4):
                queue.dma_start(out=plane[r:P:32, :].bitcast(I32), in_=by_place[r].bitcast(I32))

        def load_rows(name, src, queue):
            raw = sb.tile([P, PACK, Q], F32, name=name, align_bytes=64)
            queue.dma_start(out=raw[:], in_=src.rearrange("(p j) q -> p j q", j=PACK))
            return raw

        nc.sync.dma_start(tok[:], offs)
        nc.sync.dma_start(link[:], offs2)
        load_scales(k_scales, keys_scales, nc.scalar)
        nc.sync.dma_start(out=k_words[:].bitcast(I32), in_=keys_words[0].bitcast(I32))
        q_raw = load_rows("q_raw", query, nc.sync)
        dq_raw = load_rows("dq_raw", dquery, nc.sync)
        nc.sync.dma_start(out=v_words[:].bitcast(I32), in_=vals_words[0].bitcast(I32))
        load_scales(v_scales, vals_scales, nc.sync)
        g_raw = load_rows("g_raw", gout, nc.gpsimd)
        nc.gpsimd.dma_start(out=res[:], in_=reserve)

        def interleave(name, raw, tag):
            grouped = sb.tile([P, Q, PACK], BF16, name=name, tag=tag, align_bytes=64)
            nc.scalar.activation(grouped[:], raw[:].rearrange("p j q -> p q j"), ACT.Copy)
            return grouped

        def quantise(name, grouped, tag=None):
            codes = sb.tile([P, Q], U32, name=name + "_codes", tag=tag or name + "_codes", align_bytes=64)
            scales = sb.tile([P, Q], U8, name=name + "_scales", align_bytes=64)
            nc.vector.quantize_mx(out=codes[:].bitcast(FP8X4), scales=scales[:],
                                  in_=grouped[:].rearrange("p q j -> p (q j)"))
            return codes, scales

        def gather_packed(name, window, dtype, tag=None):
            picked = sb.tile([P, I], dtype, name=name, tag=tag or name, align_bytes=64)
            nc.vector.tensor_copy(picked[:], window[:].indirect(tok[:]))
            return picked

        def product(name, rows, words, scales):
            acc = ps.tile([Q, I], F32, name=name)
            nc.tensor.matmul_mx(out=acc[:], lhsT=rows[0][:].bitcast(FP8X4), lhsT_scale=rows[1][:],
                                rhs=words[:].bitcast(FP4X4), rhs_scale=scales[:], start=True, stop=True)
            return acc

        q_bf = interleave("q_bf", q_raw, "q_bf")
        dq_bf = interleave("dq_bf", dq_raw, "q_raw")
        g_bf = interleave("g_bf", g_raw, "dq_raw")

        kw = gather_packed("kw", k_words, U16)
        q_mx = quantise("q", q_bf)
        ks = gather_packed("ks", k_scales, U8, "q_bf")
        a = product("a", q_mx, kw, ks)
        dq_mx = quantise("dq", dq_bf, "k_words")
        ta = product("ta", dq_mx, kw, ks)
        base_sb = sb.tile([P, T], F32, name="base_sb", tag="k_words", align_bytes=64)
        nc.sync.dma_start(out=base_sb[:], in_=base)

        p, z = slots("p", "g_raw"), column("z")
        nc.scalar.activation(p[:], a[:], ACT.Exp, accum_out=z[:])
        p2 = slots("p2")
        for cols, entries in halves(link):
            nc.scalar.activation(p2[:, cols], p[:].indirect(entries), ACT.Copy)

        vw = gather_packed("vw", v_words, U16, "k_scales")
        g_mx = quantise("g", g_bf)
        vs = gather_packed("vs", v_scales, U8, "v_words")
        c0 = product("c0", g_mx, vw, vs)
        gf = sb.tile([P, T], F32, name="gf", tag="v_words", align_bytes=64)
        nc.gpsimd.memset(gf[:], 0.0)
        den = slots("den", "v_scales")
        nc.vector.scalar_tensor_tensor(den[:], p2[:], res[:], p[:], add, add)
        tp, tz = slots("tp"), column("tz")
        nc.vector.scalar_tensor_tensor(tp[:], ta[:], 1.0, p[:], mult, mult, accum_out=tz[:])

        zi, hz = column("zi"), column("hz")
        nc.vector.reciprocal(zi[:], z[:])
        dr, x, drp = slots("dr"), slots("x", "g_codes"), slots("drp")
        nc.vector.scalar_tensor_tensor(dr[:], c0[:], zi[:], p[:], mult, mult)
        nc.vector.scalar_tensor_tensor(x[:], p2[:], res[:], ta[:], add, mult)
        nc.vector.tensor_tensor(drp[:], dr[:], p[:], mult)
        nc.vector.tensor_scalar(hz[:], zi[:], 0.5, None, mult)

        rs, u = slots("rs"), slots("u")
        gp, sum_gp = slots("gp"), [column("sum_gp0"), column("sum_gp1")]
        e1, s1 = slots("e1"), slots("s1")
        v2, te1, ts1 = slots("v2"), slots("te1"), slots("ts1")
        ndz, mndz, ntdz = column("ndz"), column("mndz"), column("ntdz")
        n2, q2, sum_q2 = slots("n2"), slots("q2"), column("sum_q2")
        b2, f1, g1, f0 = (slots(n) for n in ("b2", "f1", "g1", "f0"))

        for cols, entries in halves(link):
            nc.scalar.activation(rs[:, cols], den[:, cols], ACT.Abs_reciprocal_sqrt)
        for cols, entries in halves(link):
            nc.scalar.activation(u[:, cols], rs[:, cols], ACT.Square)
        (cols0, entries0), (cols1, entries1) = halves(link)
        tp2 = sb.tile([P, HALF], F32, name="tp2", tag="rs", align_bytes=64)
        nc.scalar.activation(tp2[:], tp[:].indirect(entries0), ACT.Copy)
        for h, (cols, entries) in enumerate(halves(link)):
            nc.vector.scalar_tensor_tensor(gp[:, cols], drp[:, cols], 1.0, u[:, cols], mult, mult, accum_out=sum_gp[h][:])
        for cols, entries in halves(link):
            nc.vector.scalar_tensor_tensor(e1[:, cols], gp[:, cols], -1.0, u[:, cols], mult, mult)
            nc.scalar.activation(s1[:].indirect(entries), e1[:, cols], ACT.Copy)
        m, m2 = column("m"), column("m2")
        nc.vector.tensor_tensor(m[:], tz[:], zi[:], mult)
        ny = slots("ny", "drp")
        nc.vector.tensor_tensor(ny[:, cols0], tp2[:], x[:, cols0], sub)
        nc.vector.tensor_tensor(ny[:, cols1], tp[:].indirect(entries1), x[:, cols1], sub)
        nc.vector.tensor_tensor(m2[:], m[:], m[:], add)
        nc.vector.tensor_scalar(ndz[:], sum_gp[0][:], sum_gp[1][:], zi[:], add, mult)
        for cols, entries in halves(link):
            nc.vector.scalar_tensor_tensor(v2[:, cols], ny[:, cols], -2.0, u[:, cols], mult, mult)
        for cols, entries in halves(link):
            nc.vector.scalar_tensor_tensor(te1[:, cols], v2[:, cols], m[:], e1[:, cols], sub, mult)
            nc.scalar.activation(ts1[:].indirect(entries), te1[:, cols], ACT.Copy)
        nc.vector.scalar_tensor_tensor(n2[:], ta[:], 2.0, v2[:], mult, add)
        nc.vector.tensor_scalar(mndz[:], ndz[:], m[:], None, mult)
        nc.vector.scalar_tensor_tensor(q2[:], n2[:], m2[:], gp[:], sub, mult, accum_out=sum_q2[:])
        nc.vector.tensor_scalar(ntdz[:], sum_q2[:], hz[:], mndz[:], mult, sub)
        a2 = slots("a2", "n2")
        nc.vector.scalar_tensor_tensor(a2[:], s1[:], ndz[:], e1[:], sub, add)
        nc.vector.scalar_tensor_tensor(g1[:], te1[:], ntdz[:], p[:], sub, mult)
        nc.vector.scalar_tensor_tensor(b2[:], a2[:], 512.0, tp[:], mult, mult)
        nc.vector.tensor_tensor(f1[:], q2[:], g1[:], add)
        nc.vector.scalar_tensor_tensor(f0[:], f1[:], 512.0, b2[:], mult, add)
        b1 = slots("b1", "f1")
        nc.vector.scalar_tensor_tensor(b1[:], ts1[:], 512.0, p[:], mult, mult)
        nc.vector.tensor_tensor(gf[:].indirect(tok[:]), b1[:], f0[:], add)

        for c, (lo, hi) in enumerate(zip(OUT_EDGES, OUT_EDGES[1:])):
            cols = slice(lo, hi)
            done = sb.tile([P, hi - lo], F32, name=f"done{c}")
            nc.vector.tensor_tensor(done[:], gf[:, cols], base_sb[:, cols], add)
            nc.sync.dma_start(out=out[:, cols], in_=done[:])
